import numpy as np
import ml_dtypes


def mxq(x, axis, fmt="e4m3"):
    dtype, down = {"e4m3": (ml_dtypes.float8_e4m3fn, 7), "e5m2": (ml_dtypes.float8_e5m2, 14)}[fmt]
    v = np.moveaxis(np.asarray(x, np.float32).astype(ml_dtypes.bfloat16).astype(np.float64), axis, -1)
    blocks = v.reshape(v.shape[:-1] + (-1, 32))
    amax = np.abs(blocks).max(-1, keepdims=True)
    byte = np.maximum(np.where(amax > 0, np.frexp(amax)[1] - 1 + 127, 0) - down, 1)
    scale = np.exp2(byte - 127.0)
    codes = (blocks / scale).astype(np.float32).astype(dtype).astype(np.float64)
    return np.moveaxis((codes * scale).reshape(v.shape), -1, axis)


WIDE = False


def mx_kscale(k):
    if not WIDE:
        return np.ones(k)
    levels = np.array([30, -30])
    if k % 512:
        return np.exp2(np.random.permutation(np.resize(levels, k // 32))).repeat(32)
    a = np.empty((k // 512, 16))
    for p in range(k // 512):
        a[p, :8] = np.random.permutation(np.resize(levels, 8))
        for g in range(8):
            far = levels[np.abs(levels - a[p, g]) >= 10]
            a[p, g + 8] = far[np.random.randint(len(far))]
    return np.exp2(a.ravel()).repeat(32)


def f64(x):
    return np.asarray(x).astype(np.float64)


def striped(idx):
    return np.tile(np.asarray(idx).reshape(-1, 16).T, (8, 1)).astype(np.uint16)


def unstriped(offs):
    return offs[:16].T.reshape(-1).astype(np.int64)


E2M1 = np.array([0.0, 0.5, 1.0, 1.5, 2.0, 3.0, 4.0, 6.0, -0.0, -0.5, -1.0, -1.5, -2.0, -3.0, -4.0, -6.0])


def pack_weight(w, fmt):
    k, n = w.shape
    w = f64(np.asarray(w, np.float32).astype(ml_dtypes.bfloat16)).reshape(k // 32, 32, n)
    amax = np.abs(w).max(1)
    if fmt in ("e4m3", "e5m2"):
        byte = np.frexp(amax)[1] - 1 + 127 - (7 if fmt == "e4m3" else 14)
    else:
        mant, ex = np.frexp(amax / 6.0)
        byte = np.where(mant > 0.5, ex, ex - 1) + 127
    byte = np.clip(np.where(amax > 0, byte, 1), 1, 254)
    scaled = (w * np.exp2(127.0 - byte)[:, None, :]).reshape(k, n).astype(np.float32)
    by_word = np.ascontiguousarray(scaled.reshape(k // 512, 128, 4, n).transpose(0, 1, 3, 2))
    if fmt in ("e4m3", "e5m2"):
        words = by_word.astype(ml_dtypes.float8_e4m3fn if fmt == "e4m3" else ml_dtypes.float8_e5m2).view(np.uint8)
    else:
        c = by_word.astype(ml_dtypes.float4_e2m1fn).view(np.uint8) & 0xF
        words = (c[..., 0::2] | (c[..., 1::2] << 4)).reshape(k // 512, 128, 2 * n)
    return np.ascontiguousarray(words), np.ascontiguousarray(byte.astype(np.uint8).reshape(k // 512, 16, n))


def unpack_weight(words, scales, fmt):
    g, _, n = scales.shape
    words = np.ascontiguousarray(words).reshape(g, 128, n, -1)
    if fmt in ("e4m3", "e5m2"):
        vals = words.view(ml_dtypes.float8_e4m3fn if fmt == "e4m3" else ml_dtypes.float8_e5m2).astype(np.float64)
    else:
        nib = np.empty((g, 128, n, 4), np.uint8)
        nib[..., 0::2] = words & 0xF
        nib[..., 1::2] = words >> 4
        vals = E2M1[nib]
    vals = vals * np.repeat(np.exp2(scales.astype(np.float64) - 127.0), 8, axis=1)[..., None]
    return vals.transpose(0, 1, 3, 2).reshape(g * 512, n)


K, T, J, I, R, C, S = 512, 512, 256, 256, 512, 512, 64


def setup_inputs():
    n = np.random.standard_normal
    idx = np.random.permutation(T)[:J]
    idx2 = np.random.permutation(C)[:J]
    idx3 = np.random.permutation(T)[:I]
    fk = mx_kscale(K)
    fr = mx_kscale(R)
    xtp = pack_weight(n((K, T)) / fk[:, None], "e4m3")
    wap = pack_weight(n((K, R)) * 0.5 / np.sqrt(K) * fk[:, None] * fr, "e2m1")
    wbp = pack_weight(n((K, R)) * 1 / np.sqrt(K) * fk[:, None] / fr, "e5m2")
    return {
        "xt_words": xtp[0],
        "xt_scales": xtp[1],
        "wa_words": wap[0],
        "wa_scales": wap[1],
        "tf": (n((R, C))).astype(np.float32),
        "wb_words": wbp[0],
        "wb_scales": wbp[1],
        "cw1": (np.random.uniform(-1.0, 1.0, (1, I))).astype(np.float32),
        "offs": striped(idx),
        "offs2": striped(idx2),
        "offs3": striped(idx3),
    }


def reference(xt_words, xt_scales, wa_words, wa_scales, tf, wb_words, wb_scales, cw1, offs, offs2, offs3):
    idx = unstriped(offs)
    idx2 = unstriped(offs2)
    idx3 = unstriped(offs3)
    xtu = unpack_weight(xt_words, xt_scales, "e4m3")
    wau = unpack_weight(wa_words, wa_scales, "e2m1")
    wbu = unpack_weight(wb_words, wb_scales, "e5m2")
    xtidxg = xtu[:, idx]
    za = wau.T @ xtidxg
    ha = za * f64(tf)[:, idx2]
    xtidx3g = xtu[:, idx3]
    zb = wbu.T @ xtidx3g
    kb1 = np.max(zb, axis=1, keepdims=True)
    hb = np.maximum(zb - 0.4 * kb1, 0.0)
    haq = mxq(ha, 0, "e4m3")
    hbq = mxq(hb, 0, "e5m2")
    a0 = haq.T @ hbq
    y = 0.04 * (a0 * f64(cw1)).reshape(J, S, I // S).sum(axis=2)
    return y

@@ -1,0 +1,194 @@
+from contextlib import ExitStack
+
+import concourse.mybir as mybir
+
+K, T, J, I, R, C, S = 512, 512, 256, 256, 512, 512, 64
+FLOPS = 2 * K * R * J + 2 * K * R * I + 2 * R * J * I
+
+F32 = mybir.dt.float32
+BF16 = mybir.dt.bfloat16
+I32 = mybir.dt.int32
+U32 = mybir.dt.uint32
+U16 = mybir.dt.uint16
+U8 = mybir.dt.uint8
+E4M3 = mybir.dt.float8_e4m3fn_x4
+E5M2 = mybir.dt.float8_e5m2_x4
+E2M1 = mybir.dt.float4_e2m1fn_x4
+ALU = mybir.AluOpType
+ACT = mybir.ActivationFunctionType
+AX = mybir.AxisListType
+
+P = 128
+PACK = 4
+RUN = 8
+BLOCKS = 16
+HALF = 128
+
+
+def load_scale_rows(queue, dst, scales, quadrants):
+    rows = scales[0].bitcast(I32)
+    for q in quadrants:
+        queue.dma_start(
+            out=dst[32 * q : 32 * q + 32, :].bitcast(I32),
+            in_=rows[4 * q : 4 * q + 4, :].unsqueeze(0).broadcast_to([8, 4, T // 4]),
+        )
+
+
+def tile_list_meet_timestable_peakgated_summed_kernel(
+    tc, xt_words, xt_scales, wa_words, wa_scales, tf, wb_words, wb_scales, cw1, offs, offs2, offs3, out
+):
+    nc = tc.nc
+    with ExitStack() as ctx:
+        sb = ctx.enter_context(tc.tile_pool(name="sb", bufs=1))
+        ps = ctx.enter_context(tc.psum_pool(name="ps", bufs=1))
+
+        list_a = sb.tile([P, J // 16], U16, name="list_a")
+        list_f = sb.tile([P, J // 16], U16, name="list_f")
+        list_b = sb.tile([P, I // 16], U16, name="list_b")
+        x_words = sb.tile([P, T], U32, name="x_words", align_bytes=64)
+        x_scales = sb.tile([P, T], U8, name="x_scales", align_bytes=64)
+        wa_raw = sb.tile([P, R // 2], U32, name="wa_raw", align_bytes=64)
+        wb_raw = sb.tile([P, R], U32, name="wb_raw", align_bytes=64)
+        was_raw = sb.tile([P, R], U8, name="was_raw", align_bytes=64)
+        wbs_raw = sb.tile([P, R], U8, name="wbs_raw", align_bytes=64)
+        tf_rows = [sb.tile([P, C], F32, name="tf_rows%d" % t, tag="tf_rows%d" % t, align_bytes=64) for t in range(PACK)]
+        cw = sb.tile([P, I], F32, name="cw", align_bytes=64)
+
+        tf_dealt = tf.rearrange("(q t e) c -> t q e c", t=PACK, e=RUN)
+        nc.sync.dma_start(out=x_words[:].bitcast(I32), in_=xt_words[0].rearrange("p c r -> p (c r)").bitcast(I32))
+        nc.sync.dma_start(out=list_b[:], in_=offs3)
+        load_scale_rows(nc.sync, x_scales, xt_scales, range(4))
+        nc.sync.dma_start(out=list_a[:], in_=offs)
+        nc.sync.dma_start(out=wb_raw[:].bitcast(I32), in_=wb_words[0].rearrange("p c r -> p (c r)").bitcast(I32))
+        nc.sync.dma_start(out=list_f[:], in_=offs2)
+        load_scale_rows(nc.sync, wbs_raw, wb_scales, range(4))
+        nc.sync.dma_start(out=wa_raw[:].bitcast(I32), in_=wa_words[0].bitcast(I32))
+        load_scale_rows(nc.sync, was_raw, wa_scales, range(4))
+        for t in range(PACK):
+            nc.gpsimd.dma_start(out=tf_rows[t][:], in_=tf_dealt[t])
+        nc.sync.dma_start(out=cw[:], in_=cw1[0].partition_broadcast(P))
+
+        def deal(engine_copy, dst, src, words):
+            engine_copy(
+                out=dst.rearrange("p (t q w) -> p t q w", t=PACK, w=words),
+                in_=src.rearrange("p (q t w) -> p t q w", t=PACK, w=words),
+            )
+
+        xb_words = sb.tile([P, I], U32, name="xb_words", align_bytes=64)
+        xb_scales = sb.tile([P, I], U8, name="xb_scales", align_bytes=64)
+        wb_dealt = sb.tile([P, R], U32, name="wb_dealt", align_bytes=64)
+        wbs_dealt = sb.tile([P, R], U8, name="wbs_dealt", align_bytes=64)
+        nc.vector.tensor_copy(out=xb_words[:], in_=x_words[:].indirect(list_b[:]))
+        nc.vector.tensor_copy(out=xb_scales[:], in_=x_scales[:].indirect(list_b[:]))
+        deal(nc.vector.tensor_copy, wbs_dealt[:].bitcast(I32), wbs_raw[:].bitcast(I32), RUN // 4)
+        deal(nc.vector.tensor_copy, wb_dealt[:].bitcast(I32), wb_raw[:].bitcast(I32), RUN)
+        zb = [ps.tile([P, 2, I], F32, name="zb%d" % b) for b in range(2)]
+        for t in range(PACK):
+            cols = slice(t * P, (t + 1) * P)
+            nc.tensor.matmul_mx(
+                out=zb[t // 2][:, t % 2, :],
+                lhsT=wb_dealt[:, cols].bitcast(E5M2),
+                lhsT_scale=wbs_dealt[:, cols],
+                rhs=xb_words[:].bitcast(E4M3),
+                rhs_scale=xb_scales[:],
+                start=True,
+                stop=True,
+            )
+
+        xa_words = sb.tile([P, J], U32, name="xa_words", align_bytes=64)
+        xa_scales = sb.tile([P, J], U8, name="xa_scales", align_bytes=64)
+        wa_dealt = sb.tile([P, 2 * R], U8, name="wa_dealt", align_bytes=64)
+        was_dealt = sb.tile([P, R], U8, name="was_dealt", align_bytes=64)
+        nc.vector.tensor_copy(out=xa_words[:], in_=x_words[:].indirect(list_a[:]))
+        nc.vector.tensor_copy(out=xa_scales[:], in_=x_scales[:].indirect(list_a[:]))
+        deal(nc.vector.tensor_copy, was_dealt[:].bitcast(I32), was_raw[:].bitcast(I32), RUN // 4)
+        deal(nc.vector.tensor_copy, wa_dealt[:].bitcast(I32), wa_raw[:].bitcast(I32), RUN // 2)
+        za = [ps.tile([P, PACK, HALF], F32, name="za%d" % h) for h in range(2)]
+        for h in range(2):
+            rows = slice(h * HALF, (h + 1) * HALF)
+            for t in range(PACK):
+                nc.tensor.matmul_mx(
+                    out=za[h][:, t, :],
+                    lhsT=wa_dealt[:, 2 * t * P : 2 * (t + 1) * P].bitcast(E2M1),
+                    lhsT_scale=was_dealt[:, t * P : (t + 1) * P],
+                    rhs=xa_words[:, rows].bitcast(E4M3),
+                    rhs_scale=xa_scales[:, rows],
+                    start=True,
+                    stop=True,
+                )
+
+        factors = sb.tile([P, PACK, J], F32, name="factors", align_bytes=64)
+        for t in range(PACK):
+            nc.scalar.activation(out=factors[:, t, :], in_=tf_rows[t][:].indirect(list_f[:]), func=ACT.Copy)
+
+        peak = sb.tile([P, PACK], F32, name="peak")
+        floor = sb.tile([P, PACK], F32, name="floor")
+        hb_slots = sb.tile([P, PACK, I], BF16, name="hb_slots", tag="tf_rows3", align_bytes=64)
+        for b in range(2):
+            pair = slice(2 * b, 2 * b + 2)
+            nc.vector.tensor_reduce(out=peak[:, pair], in_=zb[b][:], axis=AX.X, op=ALU.max)
+            nc.vector.tensor_scalar(out=floor[:, pair], in0=peak[:, pair], scalar1=-0.4, scalar2=None, op0=ALU.mult)
+        for t in range(PACK):
+            nc.scalar.activation(
+                out=hb_slots[:, t, :], in_=zb[t // 2][:, t % 2, :], func=ACT.Relu, bias=floor[:, t : t + 1]
+            )
+
+        ha_in = [sb.tile([P, HALF, PACK], BF16, name="ha_in%d" % h, align_bytes=64) for h in range(2)]
+        ha_words = sb.tile([P, J], U32, name="ha_words", align_bytes=64)
+        ha_scales = sb.tile([P, J], U8, name="ha_scales", align_bytes=64)
+        for h in range(2):
+            rows = slice(h * HALF, (h + 1) * HALF)
+            nc.vector.tensor_tensor(
+                out=ha_in[h][:].rearrange("p (c i) t -> p c t i", i=4),
+                in0=za[h][:].rearrange("p t (c i) -> p c t i", i=4),
+                in1=factors[:, :, rows].rearrange("p t (c i) -> p c t i", i=4),
+                op=ALU.mult,
+            )
+        for h in range(2):
+            rows = slice(h * HALF, (h + 1) * HALF)
+            nc.vector.quantize_mx(
+                out=ha_words[:, rows].bitcast(E4M3),
+                scales=ha_scales[:, rows],
+                in_=ha_in[h][:].rearrange("p j t -> p (j t)"),
+            )
+
+        hb_in = [sb.tile([P, HALF, PACK], BF16, name="hb_in%d" % h, align_bytes=64) for h in range(2)]
+        hb_words = sb.tile([P, I], U32, name="hb_words", align_bytes=64)
+        hb_scales = sb.tile([P, I], U8, name="hb_scales", align_bytes=64)
+        for h in range(2):
+            cols = slice(h * HALF, (h + 1) * HALF)
+            nc.vector.tensor_copy(
+                out=hb_in[h][:].rearrange("p (c i) t -> p c t i", i=4),
+                in_=hb_slots[:, :, cols].rearrange("p t (c i) -> p c t i", i=4),
+            )
+        for h in range(2):
+            cols = slice(h * HALF, (h + 1) * HALF)
+            nc.vector.quantize_mx(
+                out=hb_words[:, cols].bitcast(E5M2),
+                scales=hb_scales[:, cols],
+                in_=hb_in[h][:].rearrange("p i t -> p (i t)"),
+            )
+
+        scores = [ps.tile([P, I], F32, name="scores%d" % h) for h in range(2)]
+        weighted = [sb.tile([P, I], F32, name="weighted%d" % h) for h in range(2)]
+        result = sb.tile([P, 2, S], F32, name="result")
+        for h in range(2):
+            rows = slice(h * HALF, (h + 1) * HALF)
+            nc.tensor.matmul_mx(
+                out=scores[h][:],
+                lhsT=ha_words[:, rows].bitcast(E4M3),
+                lhsT_scale=ha_scales[:, rows],
+                rhs=hb_words[:].bitcast(E5M2),
+                rhs_scale=hb_scales[:],
+                start=True,
+                stop=True,
+            )
+        for h in range(2):
+            nc.vector.scalar_tensor_tensor(
+                out=weighted[h][:], in0=scores[h][:], scalar=0.04, in1=cw[:], op0=ALU.mult, op1=ALU.mult
+            )
+        for h in range(2):
+            nc.vector.tensor_reduce(
+                out=result[:, h, :], in_=weighted[h][:].rearrange("p (s u) -> p s u", u=I // S), axis=AX.X, op=ALU.add
+            )
+        nc.sync.dma_start(out=out.rearrange("(h p) s -> p h s", p=P), in_=result[:])

@@ -47,31 +47,34 @@ def tile_list_meet_timestable_peakgated_summed_kernel(
         list_b = sb.tile([P, I // 16], U16, name="list_b")
         x_words = sb.tile([P, T], U32, name="x_words", align_bytes=64)
         x_scales = sb.tile([P, T], U8, name="x_scales", align_bytes=64)
-        wa_raw = sb.tile([P, R // 2], U32, name="wa_raw", align_bytes=64)
+        wa_raw = sb.tile([P, R // 2], U32, name="wa_raw", tag="wa_raw", align_bytes=64)
         wb_raw = sb.tile([P, R], U32, name="wb_raw", align_bytes=64)
-        was_raw = sb.tile([P, R], U8, name="was_raw", align_bytes=64)
-        wbs_raw = sb.tile([P, R], U8, name="wbs_raw", align_bytes=64)
-        tf_rows = [sb.tile([P, C], F32, name="tf_rows%d" % t, tag="tf_rows%d" % t, align_bytes=64) for t in range(PACK)]
+        was_raw = sb.tile([P, R], U8, name="was_raw", tag="was_raw", align_bytes=64)
+        wbs_raw = sb.tile([P, R], U8, name="wbs_raw", tag="wbs_raw", align_bytes=64)
+        tf_rows = [sb.tile([P, 2, C], F32, name="tf_rows%d" % u, tag="tf_rows%d" % u, align_bytes=64) for u in range(2)]
         cw = sb.tile([P, I], F32, name="cw", align_bytes=64)
 
-        tf_dealt = tf.rearrange("(q t e) c -> t q e c", t=PACK, e=RUN)
-        nc.sync.dma_start(out=x_words[:].bitcast(I32), in_=xt_words[0].rearrange("p c r -> p (c r)").bitcast(I32))
+        tf_dealt = tf.rearrange("(p u v) c -> u p v c", u=2, v=2)
         nc.sync.dma_start(out=list_b[:], in_=offs3)
-        load_scale_rows(nc.sync, x_scales, xt_scales, range(4))
+        nc.scalar.dma_start(out=x_words[:].bitcast(I32), in_=xt_words[0].rearrange("p c r -> p (c r)").bitcast(I32))
+        load_scale_rows(nc.sync, x_scales, xt_scales, (0,))
+        load_scale_rows(nc.scalar, x_scales, xt_scales, (1,))
+        load_scale_rows(nc.sync, x_scales, xt_scales, (2,))
+        load_scale_rows(nc.scalar, x_scales, xt_scales, (3,))
         nc.sync.dma_start(out=list_a[:], in_=offs)
+        nc.scalar.dma_start(out=tf_rows[0][:], in_=tf_dealt[0])
         nc.sync.dma_start(out=wb_raw[:].bitcast(I32), in_=wb_words[0].rearrange("p c r -> p (c r)").bitcast(I32))
         nc.sync.dma_start(out=list_f[:], in_=offs2)
         load_scale_rows(nc.sync, wbs_raw, wb_scales, range(4))
+        nc.sync.dma_start(out=tf_rows[1][:], in_=tf_dealt[1])
         nc.sync.dma_start(out=wa_raw[:].bitcast(I32), in_=wa_words[0].bitcast(I32))
-        load_scale_rows(nc.sync, was_raw, wa_scales, range(4))
-        for t in range(PACK):
-            nc.gpsimd.dma_start(out=tf_rows[t][:], in_=tf_dealt[t])
         nc.sync.dma_start(out=cw[:], in_=cw1[0].partition_broadcast(P))
+        load_scale_rows(nc.gpsimd, was_raw, wa_scales, range(4))
 
-        def deal(engine_copy, dst, src, words):
-            engine_copy(
-                out=dst.rearrange("p (t q w) -> p t q w", t=PACK, w=words),
-                in_=src.rearrange("p (q t w) -> p t q w", t=PACK, w=words),
+        def deal(dst, src):
+            nc.vector.tensor_copy(
+                out=dst.rearrange("p (t m) -> p t m", t=PACK),
+                in_=src.rearrange("p (m t) -> p t m", t=PACK),
             )
 
         xb_words = sb.tile([P, I], U32, name="xb_words", align_bytes=64)
@@ -80,13 +83,16 @@ def tile_list_meet_timestable_peakgated_summed_kernel(
         wbs_dealt = sb.tile([P, R], U8, name="wbs_dealt", align_bytes=64)
         nc.vector.tensor_copy(out=xb_words[:], in_=x_words[:].indirect(list_b[:]))
         nc.vector.tensor_copy(out=xb_scales[:], in_=x_scales[:].indirect(list_b[:]))
-        deal(nc.vector.tensor_copy, wbs_dealt[:].bitcast(I32), wbs_raw[:].bitcast(I32), RUN // 4)
-        deal(nc.vector.tensor_copy, wb_dealt[:].bitcast(I32), wb_raw[:].bitcast(I32), RUN)
-        zb = [ps.tile([P, 2, I], F32, name="zb%d" % b) for b in range(2)]
+        deal(wbs_dealt[:], wbs_raw[:])
+        nc.scalar.copy(
+            out=wb_dealt[:].rearrange("p (t c i) -> p c t i", t=PACK, i=4),
+            in_=wb_raw[:].rearrange("p (c i t) -> p c t i", t=PACK, i=4),
+        )
+        zb = [ps.tile([P, I], F32, name="zb%d" % t) for t in range(PACK)]
         for t in range(PACK):
             cols = slice(t * P, (t + 1) * P)
             nc.tensor.matmul_mx(
-                out=zb[t // 2][:, t % 2, :],
+                out=zb[t][:],
                 lhsT=wb_dealt[:, cols].bitcast(E5M2),
                 lhsT_scale=wbs_dealt[:, cols],
                 rhs=xb_words[:].bitcast(E4M3),
@@ -98,11 +104,11 @@ def tile_list_meet_timestable_peakgated_summed_kernel(
         xa_words = sb.tile([P, J], U32, name="xa_words", align_bytes=64)
         xa_scales = sb.tile([P, J], U8, name="xa_scales", align_bytes=64)
         wa_dealt = sb.tile([P, 2 * R], U8, name="wa_dealt", align_bytes=64)
-        was_dealt = sb.tile([P, R], U8, name="was_dealt", align_bytes=64)
+        was_dealt = sb.tile([P, R], U8, name="was_dealt", tag="wbs_raw", align_bytes=64)
         nc.vector.tensor_copy(out=xa_words[:], in_=x_words[:].indirect(list_a[:]))
         nc.vector.tensor_copy(out=xa_scales[:], in_=x_scales[:].indirect(list_a[:]))
-        deal(nc.vector.tensor_copy, was_dealt[:].bitcast(I32), was_raw[:].bitcast(I32), RUN // 4)
-        deal(nc.vector.tensor_copy, wa_dealt[:].bitcast(I32), wa_raw[:].bitcast(I32), RUN // 2)
+        deal(was_dealt[:], was_raw[:])
+        deal(wa_dealt[:].bitcast(U16), wa_raw[:].bitcast(U16))
         za = [ps.tile([P, PACK, HALF], F32, name="za%d" % h) for h in range(2)]
         for h in range(2):
             rows = slice(h * HALF, (h + 1) * HALF)
@@ -117,57 +123,48 @@ def tile_list_meet_timestable_peakgated_summed_kernel(
                     stop=True,
                 )
 
-        factors = sb.tile([P, PACK, J], F32, name="factors", align_bytes=64)
+        factors = sb.tile([P, PACK, J], F32, name="factors", tag="factors", align_bytes=64)
         for t in range(PACK):
-            nc.scalar.activation(out=factors[:, t, :], in_=tf_rows[t][:].indirect(list_f[:]), func=ACT.Copy)
+            nc.scalar.activation(out=factors[:, t, :], in_=tf_rows[t // 2][:, t % 2, :].indirect(list_f[:]), func=ACT.Copy)
 
-        peak = sb.tile([P, PACK], F32, name="peak")
         floor = sb.tile([P, PACK], F32, name="floor")
-        hb_slots = sb.tile([P, PACK, I], BF16, name="hb_slots", tag="tf_rows3", align_bytes=64)
-        for b in range(2):
-            pair = slice(2 * b, 2 * b + 2)
-            nc.vector.tensor_reduce(out=peak[:, pair], in_=zb[b][:], axis=AX.X, op=ALU.max)
-            nc.vector.tensor_scalar(out=floor[:, pair], in0=peak[:, pair], scalar1=-0.4, scalar2=None, op0=ALU.mult)
+        scaled = [
+            sb.tile([P, I], BF16, name="scaled%d" % t, tag=tag, align_bytes=64)
+            for t, tag in enumerate(("scaled", "scaled", "scaled", "wa_raw"))
+        ]
+        hb_slots = sb.tile([P, PACK, I], BF16, name="hb_slots", tag="tf_rows1", align_bytes=64)
         for t in range(PACK):
-            nc.scalar.activation(
-                out=hb_slots[:, t, :], in_=zb[t // 2][:, t % 2, :], func=ACT.Relu, bias=floor[:, t : t + 1]
+            nc.vector.tensor_scalar(
+                out=scaled[t][:], in0=zb[t][:], scalar1=-0.4, scalar2=None, op0=ALU.mult, op1=ALU.min,
+                accum_out=floor[:, t : t + 1],
             )
+        for t in range(PACK):
+            nc.scalar.activation(out=hb_slots[:, t, :], in_=zb[t][:], func=ACT.Relu, bias=floor[:, t : t + 1])
 
-        ha_in = [sb.tile([P, HALF, PACK], BF16, name="ha_in%d" % h, align_bytes=64) for h in range(2)]
+        ha_in = sb.tile([P, J, PACK], BF16, name="ha_in", align_bytes=64)
         ha_words = sb.tile([P, J], U32, name="ha_words", align_bytes=64)
         ha_scales = sb.tile([P, J], U8, name="ha_scales", align_bytes=64)
+        hb_in = sb.tile([P, I, PACK], BF16, name="hb_in", tag="factors", align_bytes=64)
+        hb_words = sb.tile([P, I], U32, name="hb_words", align_bytes=64)
+        hb_scales = sb.tile([P, I], U8, name="hb_scales", align_bytes=64)
         for h in range(2):
             rows = slice(h * HALF, (h + 1) * HALF)
             nc.vector.tensor_tensor(
-                out=ha_in[h][:].rearrange("p (c i) t -> p c t i", i=4),
+                out=ha_in[:, rows, :].rearrange("p (c i) t -> p c t i", i=4),
                 in0=za[h][:].rearrange("p t (c i) -> p c t i", i=4),
                 in1=factors[:, :, rows].rearrange("p t (c i) -> p c t i", i=4),
                 op=ALU.mult,
             )
-        for h in range(2):
-            rows = slice(h * HALF, (h + 1) * HALF)
-            nc.vector.quantize_mx(
-                out=ha_words[:, rows].bitcast(E4M3),
-                scales=ha_scales[:, rows],
-                in_=ha_in[h][:].rearrange("p j t -> p (j t)"),
-            )
-
-        hb_in = [sb.tile([P, HALF, PACK], BF16, name="hb_in%d" % h, align_bytes=64) for h in range(2)]
-        hb_words = sb.tile([P, I], U32, name="hb_words", align_bytes=64)
-        hb_scales = sb.tile([P, I], U8, name="hb_scales", align_bytes=64)
-        for h in range(2):
-            cols = slice(h * HALF, (h + 1) * HALF)
-            nc.vector.tensor_copy(
-                out=hb_in[h][:].rearrange("p (c i) t -> p c t i", i=4),
-                in_=hb_slots[:, :, cols].rearrange("p t (c i) -> p c t i", i=4),
-            )
-        for h in range(2):
-            cols = slice(h * HALF, (h + 1) * HALF)
-            nc.vector.quantize_mx(
-                out=hb_words[:, cols].bitcast(E5M2),
-                scales=hb_scales[:, cols],
-                in_=hb_in[h][:].rearrange("p i t -> p (i t)"),
-            )
+        nc.vector.tensor_copy(
+            out=hb_in[:].rearrange("p (c i) t -> p c t i", i=4),
+            in_=hb_slots[:].rearrange("p t (c i) -> p c t i", i=4),
+        )
+        nc.vector.quantize_mx(
+            out=ha_words[:].bitcast(E4M3), scales=ha_scales[:], in_=ha_in[:].rearrange("p j t -> p (j t)")
+        )
+        nc.vector.quantize_mx(
+            out=hb_words[:].bitcast(E5M2), scales=hb_scales[:], in_=hb_in[:].rearrange("p i t -> p (i t)")
+        )
 
         scores = [ps.tile([P, I], F32, name="scores%d" % h) for h in range(2)]
         weighted = [sb.tile([P, I], F32, name="weighted%d" % h) for h in range(2)]

@@ -48,33 +48,33 @@ def tile_list_meet_timestable_peakgated_summed_kernel(
         x_words = sb.tile([P, T], U32, name="x_words", align_bytes=64)
         x_scales = sb.tile([P, T], U8, name="x_scales", align_bytes=64)
         wa_raw = sb.tile([P, R // 2], U32, name="wa_raw", tag="wa_raw", align_bytes=64)
-        wb_raw = sb.tile([P, R], U32, name="wb_raw", align_bytes=64)
+        wb_raw = sb.tile([P, R], U32, name="wb_raw", tag="wb_raw", align_bytes=64)
         was_raw = sb.tile([P, R], U8, name="was_raw", tag="was_raw", align_bytes=64)
         wbs_raw = sb.tile([P, R], U8, name="wbs_raw", tag="wbs_raw", align_bytes=64)
-        tf_rows = [sb.tile([P, 2, C], F32, name="tf_rows%d" % u, tag="tf_rows%d" % u, align_bytes=64) for u in range(2)]
+        tf_rows = [sb.tile([P, C], F32, name="tf_rows%d" % t, tag="tf_rows%d" % t, align_bytes=64) for t in range(PACK)]
         cw = sb.tile([P, I], F32, name="cw", align_bytes=64)
 
-        tf_dealt = tf.rearrange("(p u v) c -> u p v c", u=2, v=2)
+        tf_dealt = tf.rearrange("(q t e) c -> t q e c", t=PACK, e=RUN)
+        load_scale_rows(nc.scalar, x_scales, xt_scales, range(4))
         nc.sync.dma_start(out=list_b[:], in_=offs3)
-        nc.scalar.dma_start(out=x_words[:].bitcast(I32), in_=xt_words[0].rearrange("p c r -> p (c r)").bitcast(I32))
-        load_scale_rows(nc.sync, x_scales, xt_scales, (0,))
-        load_scale_rows(nc.scalar, x_scales, xt_scales, (1,))
-        load_scale_rows(nc.sync, x_scales, xt_scales, (2,))
-        load_scale_rows(nc.scalar, x_scales, xt_scales, (3,))
         nc.sync.dma_start(out=list_a[:], in_=offs)
-        nc.scalar.dma_start(out=tf_rows[0][:], in_=tf_dealt[0])
+        nc.sync.dma_start(out=x_words[:].bitcast(I32), in_=xt_words[0].rearrange("p c r -> p (c r)").bitcast(I32))
         nc.sync.dma_start(out=wb_raw[:].bitcast(I32), in_=wb_words[0].rearrange("p c r -> p (c r)").bitcast(I32))
-        nc.sync.dma_start(out=list_f[:], in_=offs2)
         load_scale_rows(nc.sync, wbs_raw, wb_scales, range(4))
+        nc.sync.dma_start(out=tf_rows[0][:], in_=tf_dealt[0])
+        nc.sync.dma_start(out=list_f[:], in_=offs2)
         nc.sync.dma_start(out=tf_rows[1][:], in_=tf_dealt[1])
-        nc.sync.dma_start(out=wa_raw[:].bitcast(I32), in_=wa_words[0].bitcast(I32))
+        nc.sync.dma_start(out=tf_rows[2][:], in_=tf_dealt[2])
+        nc.gpsimd.dma_start(out=wa_raw[:].bitcast(I32), in_=wa_words[0].bitcast(I32))
+        load_scale_rows(nc.gpsimd, was_raw, wa_scales, (0,))
+        load_scale_rows(nc.sync, was_raw, wa_scales, (1, 2, 3))
+        nc.sync.dma_start(out=tf_rows[3][:], in_=tf_dealt[3])
         nc.sync.dma_start(out=cw[:], in_=cw1[0].partition_broadcast(P))
-        load_scale_rows(nc.gpsimd, was_raw, wa_scales, range(4))
 
-        def deal(dst, src):
-            nc.vector.tensor_copy(
-                out=dst.rearrange("p (t m) -> p t m", t=PACK),
-                in_=src.rearrange("p (m t) -> p t m", t=PACK),
+        def deal(engine_copy, dst, src, words):
+            engine_copy(
+                out=dst.rearrange("p (t q w) -> p t q w", t=PACK, w=words),
+                in_=src.rearrange("p (q t w) -> p t q w", t=PACK, w=words),
             )
 
         xb_words = sb.tile([P, I], U32, name="xb_words", align_bytes=64)
@@ -83,11 +83,8 @@ def tile_list_meet_timestable_peakgated_summed_kernel(
         wbs_dealt = sb.tile([P, R], U8, name="wbs_dealt", align_bytes=64)
         nc.vector.tensor_copy(out=xb_words[:], in_=x_words[:].indirect(list_b[:]))
         nc.vector.tensor_copy(out=xb_scales[:], in_=x_scales[:].indirect(list_b[:]))
-        deal(wbs_dealt[:], wbs_raw[:])
-        nc.scalar.copy(
-            out=wb_dealt[:].rearrange("p (t c i) -> p c t i", t=PACK, i=4),
-            in_=wb_raw[:].rearrange("p (c i t) -> p c t i", t=PACK, i=4),
-        )
+        deal(nc.vector.tensor_copy, wbs_dealt[:].bitcast(I32), wbs_raw[:].bitcast(I32), RUN // 4)
+        deal(nc.scalar.copy, wb_dealt[:], wb_raw[:], RUN)
         zb = [ps.tile([P, I], F32, name="zb%d" % t) for t in range(PACK)]
         for t in range(PACK):
             cols = slice(t * P, (t + 1) * P)
@@ -102,13 +99,13 @@ def tile_list_meet_timestable_peakgated_summed_kernel(
             )
 
         xa_words = sb.tile([P, J], U32, name="xa_words", align_bytes=64)
-        xa_scales = sb.tile([P, J], U8, name="xa_scales", align_bytes=64)
-        wa_dealt = sb.tile([P, 2 * R], U8, name="wa_dealt", align_bytes=64)
-        was_dealt = sb.tile([P, R], U8, name="was_dealt", tag="wbs_raw", align_bytes=64)
+        xa_scales = sb.tile([P, J], U8, name="xa_scales", tag="wbs_raw", align_bytes=64)
+        wa_dealt = sb.tile([P, 2 * R], U8, name="wa_dealt", tag="wb_raw", align_bytes=64)
+        was_dealt = sb.tile([P, R], U8, name="was_dealt", align_bytes=64)
         nc.vector.tensor_copy(out=xa_words[:], in_=x_words[:].indirect(list_a[:]))
         nc.vector.tensor_copy(out=xa_scales[:], in_=x_scales[:].indirect(list_a[:]))
-        deal(was_dealt[:], was_raw[:])
-        deal(wa_dealt[:].bitcast(U16), wa_raw[:].bitcast(U16))
+        deal(nc.vector.tensor_copy, was_dealt[:].bitcast(I32), was_raw[:].bitcast(I32), RUN // 4)
+        deal(nc.scalar.copy, wa_dealt[:].bitcast(U32), wa_raw[:], RUN // 2)
         za = [ps.tile([P, PACK, HALF], F32, name="za%d" % h) for h in range(2)]
         for h in range(2):
             rows = slice(h * HALF, (h + 1) * HALF)
@@ -124,27 +121,28 @@ def tile_list_meet_timestable_peakgated_summed_kernel(
                 )
 
         factors = sb.tile([P, PACK, J], F32, name="factors", tag="factors", align_bytes=64)
-        for t in range(PACK):
-            nc.scalar.activation(out=factors[:, t, :], in_=tf_rows[t // 2][:, t % 2, :].indirect(list_f[:]), func=ACT.Copy)
+        for t in range(PACK - 1):
+            nc.scalar.activation(out=factors[:, t, :], in_=tf_rows[t][:].indirect(list_f[:]), func=ACT.Copy)
 
         floor = sb.tile([P, PACK], F32, name="floor")
         scaled = [
-            sb.tile([P, I], BF16, name="scaled%d" % t, tag=tag, align_bytes=64)
-            for t, tag in enumerate(("scaled", "scaled", "scaled", "wa_raw"))
+            sb.tile([P, 2, I], BF16, name="scaled%d" % b, tag=tag, align_bytes=64)
+            for b, tag in enumerate(("scaled", "was_raw"))
         ]
-        hb_slots = sb.tile([P, PACK, I], BF16, name="hb_slots", tag="tf_rows1", align_bytes=64)
+        hb_slots = sb.tile([P, PACK, I], BF16, name="hb_slots", tag="tf_rows2", align_bytes=64)
         for t in range(PACK):
             nc.vector.tensor_scalar(
-                out=scaled[t][:], in0=zb[t][:], scalar1=-0.4, scalar2=None, op0=ALU.mult, op1=ALU.min,
+                out=scaled[t // 2][:, t % 2, :], in0=zb[t][:], scalar1=-0.4, scalar2=None, op0=ALU.mult, op1=ALU.min,
                 accum_out=floor[:, t : t + 1],
             )
         for t in range(PACK):
             nc.scalar.activation(out=hb_slots[:, t, :], in_=zb[t][:], func=ACT.Relu, bias=floor[:, t : t + 1])
 
+        nc.vector.tensor_copy(out=factors[:, PACK - 1, :], in_=tf_rows[PACK - 1][:].indirect(list_f[:]))
         ha_in = sb.tile([P, J, PACK], BF16, name="ha_in", align_bytes=64)
         ha_words = sb.tile([P, J], U32, name="ha_words", align_bytes=64)
         ha_scales = sb.tile([P, J], U8, name="ha_scales", align_bytes=64)
-        hb_in = sb.tile([P, I, PACK], BF16, name="hb_in", tag="factors", align_bytes=64)
+        hb_in = sb.tile([P, I, PACK], BF16, name="hb_in", align_bytes=64)
         hb_words = sb.tile([P, I], U32, name="hb_words", align_bytes=64)
         hb_scales = sb.tile([P, I], U8, name="hb_scales", align_bytes=64)
         for h in range(2):
@@ -155,13 +153,17 @@ def tile_list_meet_timestable_peakgated_summed_kernel(
                 in1=factors[:, :, rows].rearrange("p t (c i) -> p c t i", i=4),
                 op=ALU.mult,
             )
-        nc.vector.tensor_copy(
+        nc.scalar.copy(
             out=hb_in[:].rearrange("p (c i) t -> p c t i", i=4),
             in_=hb_slots[:].rearrange("p t (c i) -> p c t i", i=4),
         )
-        nc.vector.quantize_mx(
-            out=ha_words[:].bitcast(E4M3), scales=ha_scales[:], in_=ha_in[:].rearrange("p j t -> p (j t)")
-        )
+        for h in range(2):
+            rows = slice(h * HALF, (h + 1) * HALF)
+            nc.vector.quantize_mx(
+                out=ha_words[:, rows].bitcast(E4M3),
+                scales=ha_scales[:, rows],
+                in_=ha_in[:, rows, :].rearrange("p j t -> p (j t)"),
+            )
         nc.vector.quantize_mx(
             out=hb_words[:].bitcast(E5M2), scales=hb_scales[:], in_=hb_in[:].rearrange("p i t -> p (i t)")
         )

@@ -28,10 +28,7 @@ HALF = 128
 def load_scale_rows(queue, dst, scales, quadrants):
     rows = scales[0].bitcast(I32)
     for q in quadrants:
-        queue.dma_start(
-            out=dst[32 * q : 32 * q + 32, :].bitcast(I32),
-            in_=rows[4 * q : 4 * q + 4, :].unsqueeze(0).broadcast_to([8, 4, T // 4]),
-        )
+        queue.dma_start(out=dst[32 * q : 32 * q + 4, :].bitcast(I32), in_=rows[4 * q : 4 * q + 4, :])
 
 
 def tile_list_meet_timestable_peakgated_summed_kernel(
@@ -55,7 +52,14 @@ def tile_list_meet_timestable_peakgated_summed_kernel(
         cw = sb.tile([P, I], F32, name="cw", align_bytes=64)
 
         tf_dealt = tf.rearrange("(q t e) c -> t q e c", t=PACK, e=RUN)
-        load_scale_rows(nc.scalar, x_scales, xt_scales, range(4))
+        nc.vector.memset(wbs_raw[:].bitcast(I32), 0)
+        nc.vector.memset(was_raw[:].bitcast(I32), 0)
+        x_rows = xt_scales[0].bitcast(I32)
+        for q in range(4):
+            nc.scalar.dma_start(
+                out=x_scales[32 * q : 32 * q + 32, :].bitcast(I32),
+                in_=x_rows[4 * q : 4 * q + 4, :].unsqueeze(0).broadcast_to([8, 4, T // 4]),
+            )
         nc.sync.dma_start(out=list_b[:], in_=offs3)
         nc.sync.dma_start(out=list_a[:], in_=offs)
         nc.sync.dma_start(out=x_words[:].bitcast(I32), in_=xt_words[0].rearrange("p c r -> p (c r)").bitcast(I32))
@@ -121,15 +125,16 @@ def tile_list_meet_timestable_peakgated_summed_kernel(
                 )
 
         factors = sb.tile([P, PACK, J], F32, name="factors", tag="factors", align_bytes=64)
-        for t in range(PACK - 1):
+        nc.vector.tensor_copy(out=factors[:, 0, :], in_=tf_rows[0][:].indirect(list_f[:]))
+        for t in range(1, PACK):
             nc.scalar.activation(out=factors[:, t, :], in_=tf_rows[t][:].indirect(list_f[:]), func=ACT.Copy)
 
         floor = sb.tile([P, PACK], F32, name="floor")
         scaled = [
             sb.tile([P, 2, I], BF16, name="scaled%d" % b, tag=tag, align_bytes=64)
-            for b, tag in enumerate(("scaled", "was_raw"))
+            for b, tag in enumerate(("tf_rows0", "was_raw"))
         ]
-        hb_slots = sb.tile([P, PACK, I], BF16, name="hb_slots", tag="tf_rows2", align_bytes=64)
+        hb_slots = sb.tile([P, PACK, I], BF16, name="hb_slots", tag="tf_rows3", align_bytes=64)
         for t in range(PACK):
             nc.vector.tensor_scalar(
                 out=scaled[t // 2][:, t % 2, :], in0=zb[t][:], scalar1=-0.4, scalar2=None, op0=ALU.mult, op1=ALU.min,
@@ -138,7 +143,6 @@ def tile_list_meet_timestable_peakgated_summed_kernel(
         for t in range(PACK):
             nc.scalar.activation(out=hb_slots[:, t, :], in_=zb[t][:], func=ACT.Relu, bias=floor[:, t : t + 1])
 
-        nc.vector.tensor_copy(out=factors[:, PACK - 1, :], in_=tf_rows[PACK - 1][:].indirect(list_f[:]))
         ha_in = sb.tile([P, J, PACK], BF16, name="ha_in", align_bytes=64)
         ha_words = sb.tile([P, J], U32, name="ha_words", align_bytes=64)
         ha_scales = sb.tile([P, J], U8, name="ha_scales", align_bytes=64)
@@ -148,15 +152,17 @@ def tile_list_meet_timestable_peakgated_summed_kernel(
         for h in range(2):
             rows = slice(h * HALF, (h + 1) * HALF)
             nc.vector.tensor_tensor(
-                out=ha_in[:, rows, :].rearrange("p (c i) t -> p c t i", i=4),
-                in0=za[h][:].rearrange("p t (c i) -> p c t i", i=4),
-                in1=factors[:, :, rows].rearrange("p t (c i) -> p c t i", i=4),
+                out=ha_in[:, rows, :].rearrange("p (c i) t -> p c t i", i=2),
+                in0=za[h][:].rearrange("p t (c i) -> p c t i", i=2),
+                in1=factors[:, :, rows].rearrange("p t (c i) -> p c t i", i=2),
                 op=ALU.mult,
             )
-        nc.scalar.copy(
-            out=hb_in[:].rearrange("p (c i) t -> p c t i", i=4),
-            in_=hb_slots[:].rearrange("p t (c i) -> p c t i", i=4),
-        )
+        for h, engine_copy in enumerate((nc.vector.tensor_copy, nc.scalar.copy)):
+            cols = slice(h * HALF, (h + 1) * HALF)
+            engine_copy(
+                out=hb_in[:, cols, :].rearrange("p (c i) t -> p c t i", i=4),
+                in_=hb_slots[:, :, cols].rearrange("p t (c i) -> p c t i", i=4),
+            )
         for h in range(2):
             rows = slice(h * HALF, (h + 1) * HALF)
             nc.vector.quantize_mx(

@@ -69,10 +69,9 @@ def tile_list_meet_timestable_peakgated_summed_kernel(
         nc.sync.dma_start(out=list_f[:], in_=offs2)
         nc.sync.dma_start(out=tf_rows[1][:], in_=tf_dealt[1])
         nc.sync.dma_start(out=tf_rows[2][:], in_=tf_dealt[2])
+        nc.gpsimd.dma_start(out=tf_rows[3][:], in_=tf_dealt[3])
         nc.gpsimd.dma_start(out=wa_raw[:].bitcast(I32), in_=wa_words[0].bitcast(I32))
-        load_scale_rows(nc.gpsimd, was_raw, wa_scales, (0,))
-        load_scale_rows(nc.sync, was_raw, wa_scales, (1, 2, 3))
-        nc.sync.dma_start(out=tf_rows[3][:], in_=tf_dealt[3])
+        load_scale_rows(nc.sync, was_raw, wa_scales, range(4))
         nc.sync.dma_start(out=cw[:], in_=cw1[0].partition_broadcast(P))
 
         def deal(engine_copy, dst, src, words):
@@ -104,12 +103,14 @@ def tile_list_meet_timestable_peakgated_summed_kernel(
 
         xa_words = sb.tile([P, J], U32, name="xa_words", align_bytes=64)
         xa_scales = sb.tile([P, J], U8, name="xa_scales", tag="wbs_raw", align_bytes=64)
-        wa_dealt = sb.tile([P, 2 * R], U8, name="wa_dealt", tag="wb_raw", align_bytes=64)
+        wa_dealt = sb.tile([P, 2 * R], U8, name="wa_dealt", tag="tf_rows3", align_bytes=64)
         was_dealt = sb.tile([P, R], U8, name="was_dealt", align_bytes=64)
         nc.vector.tensor_copy(out=xa_words[:], in_=x_words[:].indirect(list_a[:]))
         nc.vector.tensor_copy(out=xa_scales[:], in_=x_scales[:].indirect(list_a[:]))
+        factors = sb.tile([P, PACK, J], F32, name="factors", tag="factors", align_bytes=64)
+        nc.vector.tensor_copy(out=factors[:, PACK - 1, :], in_=tf_rows[PACK - 1][:].indirect(list_f[:]))
+        deal(nc.vector.tensor_copy, wa_dealt[:].bitcast(I32), wa_raw[:].bitcast(I32), RUN // 2)
         deal(nc.vector.tensor_copy, was_dealt[:].bitcast(I32), was_raw[:].bitcast(I32), RUN // 4)
-        deal(nc.scalar.copy, wa_dealt[:].bitcast(U32), wa_raw[:], RUN // 2)
         za = [ps.tile([P, PACK, HALF], F32, name="za%d" % h) for h in range(2)]
         for h in range(2):
             rows = slice(h * HALF, (h + 1) * HALF)
@@ -124,24 +125,22 @@ def tile_list_meet_timestable_peakgated_summed_kernel(
                     stop=True,
                 )
 
-        factors = sb.tile([P, PACK, J], F32, name="factors", tag="factors", align_bytes=64)
-        nc.vector.tensor_copy(out=factors[:, 0, :], in_=tf_rows[0][:].indirect(list_f[:]))
-        for t in range(1, PACK):
+        for t in range(PACK - 1):
             nc.scalar.activation(out=factors[:, t, :], in_=tf_rows[t][:].indirect(list_f[:]), func=ACT.Copy)
 
-        floor = sb.tile([P, PACK], F32, name="floor")
-        scaled = [
-            sb.tile([P, 2, I], BF16, name="scaled%d" % b, tag=tag, align_bytes=64)
-            for b, tag in enumerate(("tf_rows0", "was_raw"))
+        floor = [
+            sb.tile([P, 2], F32, name="floor%d" % b, tag=tag, align_bytes=64)
+            for b, tag in enumerate(("wa_raw", "was_raw"))
         ]
-        hb_slots = sb.tile([P, PACK, I], BF16, name="hb_slots", tag="tf_rows3", align_bytes=64)
+        scaled = sb.tile([P, PACK, I], BF16, name="scaled", align_bytes=64)
+        hb_slots = sb.tile([P, PACK, I], BF16, name="hb_slots", tag="tf_rows2", align_bytes=64)
         for t in range(PACK):
             nc.vector.tensor_scalar(
-                out=scaled[t // 2][:, t % 2, :], in0=zb[t][:], scalar1=-0.4, scalar2=None, op0=ALU.mult, op1=ALU.min,
-                accum_out=floor[:, t : t + 1],
+                out=scaled[:, t, :], in0=zb[t][:], scalar1=-0.4, scalar2=None, op0=ALU.mult, op1=ALU.min,
+                accum_out=floor[t // 2][:, t % 2 : t % 2 + 1],
             )
         for t in range(PACK):
-            nc.scalar.activation(out=hb_slots[:, t, :], in_=zb[t][:], func=ACT.Relu, bias=floor[:, t : t + 1])
+            nc.scalar.activation(out=hb_slots[:, t, :], in_=zb[t][:], func=ACT.Relu, bias=floor[t // 2][:, t % 2 : t % 2 + 1])
 
         ha_in = sb.tile([P, J, PACK], BF16, name="ha_in", align_bytes=64)
         ha_words = sb.tile([P, J], U32, name="ha_words", align_bytes=64)

from contextlib import ExitStack

import concourse.mybir as mybir

K, T, J, I, R, C, S = 512, 512, 256, 256, 512, 512, 64
FLOPS = 2 * K * R * J + 2 * K * R * I + 2 * R * J * I

F32 = mybir.dt.float32
BF16 = mybir.dt.bfloat16
I32 = mybir.dt.int32
U32 = mybir.dt.uint32
U16 = mybir.dt.uint16
U8 = mybir.dt.uint8
E4M3 = mybir.dt.float8_e4m3fn_x4
E5M2 = mybir.dt.float8_e5m2_x4
E2M1 = mybir.dt.float4_e2m1fn_x4
ALU = mybir.AluOpType
ACT = mybir.ActivationFunctionType
AX = mybir.AxisListType

P = 128
PACK = 4
RUN = 8
BLOCKS = 16
HALF = 128


def load_scale_rows(queue, dst, scales, quadrants):
    rows = scales[0].bitcast(I32)
    for q in quadrants:
        queue.dma_start(out=dst[32 * q : 32 * q + 4, :].bitcast(I32), in_=rows[4 * q : 4 * q + 4, :])


def tile_list_meet_timestable_peakgated_summed_kernel(
    tc, xt_words, xt_scales, wa_words, wa_scales, tf, wb_words, wb_scales, cw1, offs, offs2, offs3, out
):
    nc = tc.nc
    with ExitStack() as ctx:
        sb = ctx.enter_context(tc.tile_pool(name="sb", bufs=1))
        ps = ctx.enter_context(tc.psum_pool(name="ps", bufs=1))

        list_a = sb.tile([P, J // 16], U16, name="list_a")
        list_f = sb.tile([P, J // 16], U16, name="list_f")
        list_b = sb.tile([P, I // 16], U16, name="list_b")
        x_words = sb.tile([P, T], U32, name="x_words", align_bytes=64)
        x_scales = sb.tile([P, T], U8, name="x_scales", align_bytes=64)
        wa_raw = sb.tile([P, R // 2], U32, name="wa_raw", tag="wa_raw", align_bytes=64)
        wb_raw = sb.tile([P, R], U32, name="wb_raw", tag="wb_raw", align_bytes=64)
        was_raw = sb.tile([P, R], U8, name="was_raw", tag="was_raw", align_bytes=64)
        wbs_raw = sb.tile([P, R], U8, name="wbs_raw", tag="wbs_raw", align_bytes=64)
        tf_rows = [sb.tile([P, C], F32, name="tf_rows%d" % t, tag="tf_rows%d" % t, align_bytes=64) for t in range(PACK)]
        cw = sb.tile([P, I], F32, name="cw", align_bytes=64)

        tf_dealt = tf.rearrange("(q t e) c -> t q e c", t=PACK, e=RUN)
        nc.vector.memset(wbs_raw[:].bitcast(I32), 0)
        nc.vector.memset(was_raw[:].bitcast(I32), 0)
        x_rows = xt_scales[0].bitcast(I32)
        for q in range(4):
            nc.scalar.dma_start(
                out=x_scales[32 * q : 32 * q + 32, :].bitcast(I32),
                in_=x_rows[4 * q : 4 * q + 4, :].unsqueeze(0).broadcast_to([8, 4, T // 4]),
            )
        nc.sync.dma_start(out=list_b[:], in_=offs3)
        nc.sync.dma_start(out=list_a[:], in_=offs)
        nc.sync.dma_start(out=x_words[:].bitcast(I32), in_=xt_words[0].rearrange("p c r -> p (c r)").bitcast(I32))
        nc.sync.dma_start(out=wb_raw[:].bitcast(I32), in_=wb_words[0].rearrange("p c r -> p (c r)").bitcast(I32))
        load_scale_rows(nc.sync, wbs_raw, wb_scales, range(4))
        nc.sync.dma_start(out=tf_rows[0][:], in_=tf_dealt[0])
        nc.sync.dma_start(out=list_f[:], in_=offs2)
        nc.sync.dma_start(out=tf_rows[1][:], in_=tf_dealt[1])
        nc.sync.dma_start(out=tf_rows[2][:], in_=tf_dealt[2])
        nc.gpsimd.dma_start(out=tf_rows[3][:], in_=tf_dealt[3])
        nc.gpsimd.dma_start(out=wa_raw[:].bitcast(I32), in_=wa_words[0].bitcast(I32))
        load_scale_rows(nc.sync, was_raw, wa_scales, range(4))
        nc.sync.dma_start(out=cw[:], in_=cw1[0].partition_broadcast(P))

        def deal(engine_copy, dst, src, words):
            engine_copy(
                out=dst.rearrange("p (t q w) -> p t q w", t=PACK, w=words),
                in_=src.rearrange("p (q t w) -> p t q w", t=PACK, w=words),
            )

        xb_words = sb.tile([P, I], U32, name="xb_words", align_bytes=64)
        xb_scales = sb.tile([P, I], U8, name="xb_scales", align_bytes=64)
        wb_dealt = sb.tile([P, R], U32, name="wb_dealt", align_bytes=64)
        wbs_dealt = sb.tile([P, R], U8, name="wbs_dealt", align_bytes=64)
        nc.vector.tensor_copy(out=xb_words[:], in_=x_words[:].indirect(list_b[:]))
        nc.vector.tensor_copy(out=xb_scales[:], in_=x_scales[:].indirect(list_b[:]))
        deal(nc.vector.tensor_copy, wbs_dealt[:].bitcast(I32), wbs_raw[:].bitcast(I32), RUN // 4)
        deal(nc.scalar.copy, wb_dealt[:], wb_raw[:], RUN)
        zb = [ps.tile([P, I], F32, name="zb%d" % t) for t in range(PACK)]
        for t in range(PACK):
            cols = slice(t * P, (t + 1) * P)
            nc.tensor.matmul_mx(
                out=zb[t][:],
                lhsT=wb_dealt[:, cols].bitcast(E5M2),
                lhsT_scale=wbs_dealt[:, cols],
                rhs=xb_words[:].bitcast(E4M3),
                rhs_scale=xb_scales[:],
                start=True,
                stop=True,
            )

        xa_words = sb.tile([P, J], U32, name="xa_words", align_bytes=64)
        xa_scales = sb.tile([P, J], U8, name="xa_scales", tag="wbs_raw", align_bytes=64)
        wa_dealt = sb.tile([P, 2 * R], U8, name="wa_dealt", tag="tf_rows3", align_bytes=64)
        was_dealt = sb.tile([P, R], U8, name="was_dealt", align_bytes=64)
        nc.vector.tensor_copy(out=xa_words[:], in_=x_words[:].indirect(list_a[:]))
        nc.vector.tensor_copy(out=xa_scales[:], in_=x_scales[:].indirect(list_a[:]))
        factors = sb.tile([P, PACK, J], F32, name="factors", tag="factors", align_bytes=64)
        nc.vector.tensor_copy(out=factors[:, PACK - 1, :], in_=tf_rows[PACK - 1][:].indirect(list_f[:]))
        deal(nc.vector.tensor_copy, wa_dealt[:].bitcast(I32), wa_raw[:].bitcast(I32), RUN // 2)
        deal(nc.vector.tensor_copy, was_dealt[:].bitcast(I32), was_raw[:].bitcast(I32), RUN // 4)
        za = [ps.tile([P, PACK, HALF], F32, name="za%d" % h) for h in range(2)]
        for h in range(2):
            rows = slice(h * HALF, (h + 1) * HALF)
            for t in range(PACK):
                nc.tensor.matmul_mx(
                    out=za[h][:, t, :],
                    lhsT=wa_dealt[:, 2 * t * P : 2 * (t + 1) * P].bitcast(E2M1),
                    lhsT_scale=was_dealt[:, t * P : (t + 1) * P],
                    rhs=xa_words[:, rows].bitcast(E4M3),
                    rhs_scale=xa_scales[:, rows],
                    start=True,
                    stop=True,
                )

        for t in range(PACK - 1):
            nc.scalar.activation(out=factors[:, t, :], in_=tf_rows[t][:].indirect(list_f[:]), func=ACT.Copy)

        floor = [
            sb.tile([P, 2], F32, name="floor%d" % b, tag=tag, align_bytes=64)
            for b, tag in enumerate(("wa_raw", "was_raw"))
        ]
        scaled = sb.tile([P, PACK, I], BF16, name="scaled", align_bytes=64)
        hb_slots = sb.tile([P, PACK, I], BF16, name="hb_slots", tag="tf_rows2", align_bytes=64)
        for t in range(PACK):
            nc.vector.tensor_scalar(
                out=scaled[:, t, :], in0=zb[t][:], scalar1=-0.4, scalar2=None, op0=ALU.mult, op1=ALU.min,
                accum_out=floor[t // 2][:, t % 2 : t % 2 + 1],
            )
        for t in range(PACK):
            nc.scalar.activation(out=hb_slots[:, t, :], in_=zb[t][:], func=ACT.Relu, bias=floor[t // 2][:, t % 2 : t % 2 + 1])

        ha_in = sb.tile([P, J, PACK], BF16, name="ha_in", align_bytes=64)
        ha_words = sb.tile([P, J], U32, name="ha_words", align_bytes=64)
        ha_scales = sb.tile([P, J], U8, name="ha_scales", align_bytes=64)
        hb_in = sb.tile([P, I, PACK], BF16, name="hb_in", align_bytes=64)
        hb_words = sb.tile([P, I], U32, name="hb_words", align_bytes=64)
        hb_scales = sb.tile([P, I], U8, name="hb_scales", align_bytes=64)
        for h in range(2):
            rows = slice(h * HALF, (h + 1) * HALF)
            nc.vector.tensor_tensor(
                out=ha_in[:, rows, :].rearrange("p (c i) t -> p c t i", i=2),
                in0=za[h][:].rearrange("p t (c i) -> p c t i", i=2),
                in1=factors[:, :, rows].rearrange("p t (c i) -> p c t i", i=2),
                op=ALU.mult,
            )
        for h, engine_copy in enumerate((nc.vector.tensor_copy, nc.scalar.copy)):
            cols = slice(h * HALF, (h + 1) * HALF)
            engine_copy(
                out=hb_in[:, cols, :].rearrange("p (c i) t -> p c t i", i=4),
                in_=hb_slots[:, :, cols].rearrange("p t (c i) -> p c t i", i=4),
            )
        for h in range(2):
            rows = slice(h * HALF, (h + 1) * HALF)
            nc.vector.quantize_mx(
                out=ha_words[:, rows].bitcast(E4M3),
                scales=ha_scales[:, rows],
                in_=ha_in[:, rows, :].rearrange("p j t -> p (j t)"),
            )
        nc.vector.quantize_mx(
            out=hb_words[:].bitcast(E5M2), scales=hb_scales[:], in_=hb_in[:].rearrange("p i t -> p (i t)")
        )

        scores = [ps.tile([P, I], F32, name="scores%d" % h) for h in range(2)]
        weighted = [sb.tile([P, I], F32, name="weighted%d" % h) for h in range(2)]
        result = sb.tile([P, 2, S], F32, name="result")
        for h in range(2):
            rows = slice(h * HALF, (h + 1) * HALF)
            nc.tensor.matmul_mx(
                out=scores[h][:],
                lhsT=ha_words[:, rows].bitcast(E4M3),
                lhsT_scale=ha_scales[:, rows],
                rhs=hb_words[:].bitcast(E5M2),
                rhs_scale=hb_scales[:],
                start=True,
                stop=True,
            )
        for h in range(2):
            nc.vector.scalar_tensor_tensor(
                out=weighted[h][:], in0=scores[h][:], scalar=0.04, in1=cw[:], op0=ALU.mult, op1=ALU.mult
            )
        for h in range(2):
            nc.vector.tensor_reduce(
                out=result[:, h, :], in_=weighted[h][:].rearrange("p (s u) -> p s u", u=I // S), axis=AX.X, op=ALU.add
            )
        nc.sync.dma_start(out=out.rearrange("(h p) s -> p h s", p=P), in_=result[:])
